import numpy as np
import ml_dtypes


def mxq(x, axis, fmt="e4m3"):
    dtype, down = {"e4m3": (ml_dtypes.float8_e4m3fn, 7), "e5m2": (ml_dtypes.float8_e5m2, 14)}[fmt]
    v = np.moveaxis(np.asarray(x, np.float32).astype(ml_dtypes.bfloat16).astype(np.float64), axis, -1)
    blocks = v.reshape(v.shape[:-1] + (-1, 32))
    amax = np.abs(blocks).max(-1, keepdims=True)
    byte = np.maximum(np.where(amax > 0, np.frexp(amax)[1] - 1 + 127, 0) - down, 1)
    scale = np.exp2(byte - 127.0)
    codes = (blocks / scale).astype(np.float32).astype(dtype).astype(np.float64)
    return np.moveaxis((codes * scale).reshape(v.shape), -1, axis)


WIDE = False


def mx_kscale(k):
    if not WIDE:
        return np.ones(k)
    levels = np.array([10, -10, 5, -5, 0])
    if k % 512:
        return np.exp2(np.random.permutation(np.resize(levels, k // 32))).repeat(32)
    a = np.empty((k // 512, 16))
    for p in range(k // 512):
        a[p, :8] = np.random.permutation(np.resize(levels, 8))
        for g in range(8):
            far = levels[np.abs(levels - a[p, g]) >= 10]
            a[p, g + 8] = far[np.random.randint(len(far))]
    return np.exp2(a.ravel()).repeat(32)


def f64(x):
    return np.asarray(x).astype(np.float64)


def striped(idx):
    return np.tile(idx.reshape(-1, 16).T, (8, 1)).astype(np.uint16)


def unstriped(offs):
    return offs[:16].T.reshape(-1).astype(np.int64)


E2M1 = np.array([0.0, 0.5, 1.0, 1.5, 2.0, 3.0, 4.0, 6.0, -0.0, -0.5, -1.0, -1.5, -2.0, -3.0, -4.0, -6.0])


def pack_weight(w, fmt):
    k, n = w.shape
    w = f64(np.asarray(w, np.float32).astype(ml_dtypes.bfloat16)).reshape(k // 32, 32, n)
    amax = np.abs(w).max(1)
    if fmt == "e4m3":
        byte = np.frexp(amax)[1] - 1 + 127 - 7
    else:
        mant, ex = np.frexp(amax / 6.0)
        byte = np.where(mant > 0.5, ex, ex - 1) + 127
    byte = np.clip(np.where(amax > 0, byte, 1), 1, 254)
    scaled = (w * np.exp2(127.0 - byte)[:, None, :]).reshape(k, n).astype(np.float32)
    by_word = np.ascontiguousarray(scaled.reshape(k // 512, 128, 4, n).transpose(0, 1, 3, 2))
    if fmt == "e4m3":
        words = by_word.astype(ml_dtypes.float8_e4m3fn).view(np.uint8)
    else:
        c = by_word.astype(ml_dtypes.float4_e2m1fn).view(np.uint8) & 0xF
        words = (c[..., 0::2] | (c[..., 1::2] << 4)).reshape(k // 512, 128, 2 * n)
    return np.ascontiguousarray(words), np.ascontiguousarray(byte.astype(np.uint8).reshape(k // 512, 16, n))


def unpack_weight(words, scales, fmt):
    g, _, n = scales.shape
    words = np.ascontiguousarray(words).reshape(g, 128, n, -1)
    if fmt == "e4m3":
        vals = words.view(ml_dtypes.float8_e4m3fn).astype(np.float64)
    else:
        nib = np.empty((g, 128, n, 4), np.uint8)
        nib[..., 0::2] = words & 0xF
        nib[..., 1::2] = words >> 4
        vals = E2M1[nib]
    vals = vals * np.repeat(np.exp2(scales.astype(np.float64) - 127.0), 8, axis=1)[..., None]
    return vals.transpose(0, 1, 3, 2).reshape(g * 512, n)


def gelu(v):
    return 0.5 * v * (1.0 + np.tanh(np.sqrt(2.0 / np.pi) * (v + 0.044715 * v**3)))


K, M, T, S = 1024, 128, 4096, 1536


def setup_inputs():
    n = np.random.standard_normal
    s = mx_kscale(K)[:, None]
    v = pack_weight(n((K, T)) * s, "e4m3")
    return {
        "tab_words": v[0],
        "tab_scales": v[1],
        "w": (n((K, M)) / np.sqrt(K) / s).astype(np.float32),
        "rT": n((M, T)).astype(np.float32),
        "b": (0.3 * n(128)).astype(np.float32),
        "offs": striped(np.random.permutation(T)[:S]),
    }


def reference(tab_words, tab_scales, w, rT, b, offs):
    tab_ = unpack_weight(tab_words, tab_scales, "e4m3")[:, unstriped(offs)]
    w_ = mxq(f64(w), 0, "e4m3")
    y = w_.T @ tab_
    return (gelu(y + f64(b)[:, None])) + f64(rT)[:, unstriped(offs)]

@@ -1,0 +1,123 @@
+from contextlib import ExitStack
+
+import concourse.mybir as mybir
+
+K, M, T, S = 1024, 128, 4096, 1536
+FLOPS = 2 * K * M * S
+
+F32 = mybir.dt.float32
+BF16 = mybir.dt.bfloat16
+I32 = mybir.dt.int32
+U32 = mybir.dt.uint32
+U16 = mybir.dt.uint16
+U8 = mybir.dt.uint8
+FP8X4 = mybir.dt.float8_e4m3fn_x4
+
+P = 128
+PACK = 4
+PASSES = K // (P * PACK)
+N_TILE = 512
+TILES = S // N_TILE
+OFFS_COLS = N_TILE // 16
+ROWS = 4
+
+
+def tile_list_tabres_gelu_kernel(tc, tab_words, tab_scales, w, rT, b, offs, out):
+    nc = tc.nc
+    with ExitStack() as ctx:
+        keep = ctx.enter_context(tc.tile_pool(name="keep", bufs=1))
+        psum = ctx.enter_context(tc.psum_pool(name="psum", bufs=1))
+
+        offsets = keep.tile([P, S // 16], U16, name="offsets")
+        words = [keep.tile([P, T], I32, name="words%d" % a, align_bytes=64) for a in range(PASSES)]
+        scale_tab = keep.tile([P, T // 4], I32, name="scale_tab", align_bytes=64)
+        resid = keep.tile([P, T], F32, name="resid", align_bytes=64)
+        w_raw = keep.tile([P, PASSES, PACK, M], F32, name="w_raw", align_bytes=64)
+        bias = keep.tile([P, 1], F32, name="bias")
+
+        nc.sync.dma_start(offsets[:], offs)
+        nc.sync.dma_start(out=words[0][:], in_=tab_words[0].rearrange("p t i -> p (t i)").bitcast(I32))
+        nc.sync.dma_start(
+            out=w_raw[:].rearrange("p a j n -> p a (j n)"),
+            in_=w.rearrange("(a p j) n -> p a (j n)", a=PASSES, j=PACK),
+        )
+        nc.sync.dma_start(out=words[1][:], in_=tab_words[1].rearrange("p t i -> p (t i)").bitcast(I32))
+        nc.sync.dma_start(out=resid[:], in_=rT)
+        nc.scalar.dma_start(out=bias[:], in_=b.rearrange("(p o) -> p o", o=1))
+
+        nc.vector.memset(scale_tab[:], 0)
+        for q in range(4):
+            nc.gpsimd.dma_start(
+                out=scale_tab[32 * q : 32 * q + ROWS * PASSES, :],
+                in_=tab_scales[:, ROWS * q : ROWS * (q + 1), :].bitcast(I32),
+            )
+
+        def cols(i):
+            return slice(i * N_TILE, (i + 1) * N_TILE)
+
+        def offs_of(i):
+            return offsets[:, i * OFFS_COLS : (i + 1) * OFFS_COLS]
+
+        picked = [keep.tile([P, S], U32, name="picked%d" % a, align_bytes=64) for a in range(PASSES)]
+        picked_scales = keep.tile([P, S], U8, name="picked_scales", align_bytes=64)
+
+        nc.vector.tensor_copy(picked[0][:], words[0][:].bitcast(U32).indirect(offsets[:]))
+        for i in range(TILES):
+            nc.vector.tensor_copy(picked_scales[:, cols(i)], scale_tab[:].bitcast(U8).indirect(offs_of(i)))
+
+        w_bf = keep.tile([P, PASSES, M, PACK], BF16, name="w_bf", align_bytes=64)
+        nc.scalar.copy(out=w_bf[:], in_=w_raw[:].rearrange("p a j n -> p a n j"))
+        w_codes = keep.tile([P, PASSES * M], U32, name="w_codes", align_bytes=64)
+        w_scales = keep.tile([P, PASSES * M], U8, name="w_scales", align_bytes=64)
+        nc.vector.quantize_mx(
+            out=w_codes[:].bitcast(FP8X4),
+            scales=w_scales[:],
+            in_=w_bf[:].rearrange("p a n j -> p (a n j)"),
+        )
+
+        acc = [psum.tile([M, N_TILE], F32, name="acc%d" % i) for i in range(TILES)]
+
+        def mx_pass(a, i):
+            nc.tensor.matmul_mx(
+                out=acc[i][:],
+                lhsT=w_codes[:, a * M : (a + 1) * M].bitcast(FP8X4),
+                lhsT_scale=w_scales[:, a * M : (a + 1) * M],
+                rhs=picked[a][:, cols(i)].bitcast(FP8X4),
+                rhs_scale=picked_scales[ROWS * a : P, cols(i)],
+                start=(a == 0),
+                stop=(a == PASSES - 1),
+            )
+
+        for i in range(TILES):
+            mx_pass(0, i)
+
+        act = [keep.tile([M, N_TILE], F32, name="act%d" % i) for i in range(TILES)]
+        for i in range(TILES):
+            nc.vector.tensor_copy(picked[1][:, cols(i)], words[1][:].bitcast(U32).indirect(offs_of(i)))
+            mx_pass(1, i)
+            nc.scalar.activation(
+                out=act[i][:],
+                in_=acc[i][:],
+                func=mybir.ActivationFunctionType.Gelu_apprx_tanh,
+                bias=bias[:],
+            )
+
+        picked_resid = [keep.tile([M, N_TILE], F32, name="picked_resid%d" % i) for i in range(TILES)]
+        result = [keep.tile([M, N_TILE], F32, name="result%d" % i) for i in range(TILES)]
+
+        def gather_resid(i):
+            nc.vector.tensor_copy(picked_resid[i][:], resid[:].indirect(offs_of(i)))
+
+        def add_and_store(i, lo, hi, queue):
+            nc.vector.tensor_tensor(
+                result[i][:, lo:hi], picked_resid[i][:, lo:hi], act[i][:, lo:hi], mybir.AluOpType.add
+            )
+            queue.dma_start(out=out[:, i * N_TILE + lo : i * N_TILE + hi], in_=result[i][:, lo:hi])
+
+        gather_resid(0)
+        gather_resid(1)
+        add_and_store(0, 0, N_TILE, nc.sync)
+        gather_resid(2)
+        add_and_store(1, 0, N_TILE, nc.sync)
+        add_and_store(2, 0, N_TILE // 2, nc.scalar)
+        add_and_store(2, N_TILE // 2, N_TILE, nc.sync)

@@ -20,12 +20,14 @@ N_TILE = 512
 TILES = S // N_TILE
 OFFS_COLS = N_TILE // 16
 ROWS = 4
+HEAD = 1280
 
 
 def tile_list_tabres_gelu_kernel(tc, tab_words, tab_scales, w, rT, b, offs, out):
     nc = tc.nc
     with ExitStack() as ctx:
         keep = ctx.enter_context(tc.tile_pool(name="keep", bufs=1))
+        ring = ctx.enter_context(tc.tile_pool(name="ring", bufs=2))
         psum = ctx.enter_context(tc.psum_pool(name="psum", bufs=1))
 
         offsets = keep.tile([P, S // 16], U16, name="offsets")
@@ -35,22 +37,29 @@ def tile_list_tabres_gelu_kernel(tc, tab_words, tab_scales, w, rT, b, offs, out)
         w_raw = keep.tile([P, PASSES, PACK, M], F32, name="w_raw", align_bytes=64)
         bias = keep.tile([P, 1], F32, name="bias")
 
-        nc.sync.dma_start(offsets[:], offs)
-        nc.sync.dma_start(out=words[0][:], in_=tab_words[0].rearrange("p t i -> p (t i)").bitcast(I32))
-        nc.sync.dma_start(
-            out=w_raw[:].rearrange("p a j n -> p a (j n)"),
-            in_=w.rearrange("(a p j) n -> p a (j n)", a=PASSES, j=PACK),
-        )
-        nc.sync.dma_start(out=words[1][:], in_=tab_words[1].rearrange("p t i -> p (t i)").bitcast(I32))
-        nc.sync.dma_start(out=resid[:], in_=rT)
-        nc.scalar.dma_start(out=bias[:], in_=b.rearrange("(p o) -> p o", o=1))
+        def load_words(a, lo, hi):
+            rows = tab_words[a].rearrange("p t i -> p (t i)").bitcast(I32)
+            nc.sync.dma_start(out=words[a][:, lo:hi], in_=rows[:, lo:hi])
+
+        def load_scales(a):
+            for r in range(ROWS):
+                nc.sync.dma_start(
+                    out=scale_tab[ROWS * a + r : P : 32, :],
+                    in_=tab_scales[a, r : 16 : ROWS, :].bitcast(I32),
+                )
 
         nc.vector.memset(scale_tab[:], 0)
-        for q in range(4):
-            nc.gpsimd.dma_start(
-                out=scale_tab[32 * q : 32 * q + ROWS * PASSES, :],
-                in_=tab_scales[:, ROWS * q : ROWS * (q + 1), :].bitcast(I32),
-            )
+        nc.sync.dma_start(offsets[:], offs)
+        w_rows = w.rearrange("(a p j) n -> a p (j n)", a=PASSES, j=PACK)
+        for a in range(PASSES):
+            nc.sync.dma_start(out=w_raw[:, a].rearrange("p j n -> p (j n)"), in_=w_rows[a])
+        load_scales(0)
+        load_words(0, 0, HEAD)
+        load_scales(1)
+        load_words(0, HEAD, T)
+        nc.sync.dma_start(out=bias[:], in_=b.rearrange("(p o) -> p o", o=1))
+        load_words(1, 0, T)
+        nc.sync.dma_start(out=resid[:], in_=rT)
 
         def cols(i):
             return slice(i * N_TILE, (i + 1) * N_TILE)
@@ -61,12 +70,8 @@ def tile_list_tabres_gelu_kernel(tc, tab_words, tab_scales, w, rT, b, offs, out)
         picked = [keep.tile([P, S], U32, name="picked%d" % a, align_bytes=64) for a in range(PASSES)]
         picked_scales = keep.tile([P, S], U8, name="picked_scales", align_bytes=64)
 
-        nc.vector.tensor_copy(picked[0][:], words[0][:].bitcast(U32).indirect(offsets[:]))
-        for i in range(TILES):
-            nc.vector.tensor_copy(picked_scales[:, cols(i)], scale_tab[:].bitcast(U8).indirect(offs_of(i)))
-
         w_bf = keep.tile([P, PASSES, M, PACK], BF16, name="w_bf", align_bytes=64)
-        nc.scalar.copy(out=w_bf[:], in_=w_raw[:].rearrange("p a j n -> p a n j"))
+        nc.vector.tensor_copy(out=w_bf[:], in_=w_raw[:].rearrange("p a j n -> p a n j"))
         w_codes = keep.tile([P, PASSES * M], U32, name="w_codes", align_bytes=64)
         w_scales = keep.tile([P, PASSES * M], U8, name="w_scales", align_bytes=64)
         nc.vector.quantize_mx(
@@ -74,6 +79,10 @@ def tile_list_tabres_gelu_kernel(tc, tab_words, tab_scales, w, rT, b, offs, out)
             scales=w_scales[:],
             in_=w_bf[:].rearrange("p a n j -> p (a n j)"),
         )
+
+        for i in range(TILES):
+            nc.vector.tensor_copy(picked_scales[:, cols(i)], scale_tab[:].bitcast(U8).indirect(offs_of(i)))
+        nc.vector.tensor_copy(picked[0][:], words[0][:].bitcast(U32).indirect(offsets[:]))
 
         acc = [psum.tile([M, N_TILE], F32, name="acc%d" % i) for i in range(TILES)]
 
@@ -102,10 +111,11 @@ def tile_list_tabres_gelu_kernel(tc, tab_words, tab_scales, w, rT, b, offs, out)
                 bias=bias[:],
             )
 
-        picked_resid = [keep.tile([M, N_TILE], F32, name="picked_resid%d" % i) for i in range(TILES)]
+        picked_resid = {}
         result = [keep.tile([M, N_TILE], F32, name="result%d" % i) for i in range(TILES)]
 
         def gather_resid(i):
+            picked_resid[i] = ring.tile([M, N_TILE], F32, name="picked_resid")
             nc.vector.tensor_copy(picked_resid[i][:], resid[:].indirect(offs_of(i)))
 
         def add_and_store(i, lo, hi, queue):

@@ -20,7 +20,7 @@ N_TILE = 512
 TILES = S // N_TILE
 OFFS_COLS = N_TILE // 16
 ROWS = 4
-HEAD = 1280
+HEAD = 1536
 
 
 def tile_list_tabres_gelu_kernel(tc, tab_words, tab_scales, w, rT, b, offs, out):
@@ -41,25 +41,31 @@ def tile_list_tabres_gelu_kernel(tc, tab_words, tab_scales, w, rT, b, offs, out)
             rows = tab_words[a].rearrange("p t i -> p (t i)").bitcast(I32)
             nc.sync.dma_start(out=words[a][:, lo:hi], in_=rows[:, lo:hi])
 
-        def load_scales(a):
-            for r in range(ROWS):
-                nc.sync.dma_start(
-                    out=scale_tab[ROWS * a + r : P : 32, :],
-                    in_=tab_scales[a, r : 16 : ROWS, :].bitcast(I32),
-                )
+        def load_scales(rows):
+            for r in rows:
+                for a in range(PASSES):
+                    nc.sync.dma_start(
+                        out=scale_tab[ROWS * a + r : P : 32, :],
+                        in_=tab_scales[a, r : 16 : ROWS, :].bitcast(I32),
+                    )
 
         nc.vector.memset(scale_tab[:], 0)
         nc.sync.dma_start(offsets[:], offs)
         w_rows = w.rearrange("(a p j) n -> a p (j n)", a=PASSES, j=PACK)
         for a in range(PASSES):
             nc.sync.dma_start(out=w_raw[:, a].rearrange("p j n -> p (j n)"), in_=w_rows[a])
-        load_scales(0)
+        load_scales((0, 1))
         load_words(0, 0, HEAD)
-        load_scales(1)
+        load_scales((2, 3))
         load_words(0, HEAD, T)
-        nc.sync.dma_start(out=bias[:], in_=b.rearrange("(p o) -> p o", o=1))
         load_words(1, 0, T)
         nc.sync.dma_start(out=resid[:], in_=rT)
+        nc.sync.dma_start(out=bias[:], in_=b.rearrange("(p o) -> p o", o=1))
+
+        warm_in = keep.tile([P, 1], F32, name="warm_in")
+        warm_out = keep.tile([P, 1], F32, name="warm_out")
+        nc.vector.memset(warm_in[:], 0.0)
+        nc.scalar.activation(out=warm_out[:], in_=warm_in[:], func=mybir.ActivationFunctionType.Gelu_apprx_tanh)
 
         def cols(i):
             return slice(i * N_TILE, (i + 1) * N_TILE)

@@ -20,14 +20,13 @@ N_TILE = 512
 TILES = S // N_TILE
 OFFS_COLS = N_TILE // 16
 ROWS = 4
-HEAD = 1536
+HEAD = 1024
 
 
 def tile_list_tabres_gelu_kernel(tc, tab_words, tab_scales, w, rT, b, offs, out):
     nc = tc.nc
     with ExitStack() as ctx:
         keep = ctx.enter_context(tc.tile_pool(name="keep", bufs=1))
-        ring = ctx.enter_context(tc.tile_pool(name="ring", bufs=2))
         psum = ctx.enter_context(tc.psum_pool(name="psum", bufs=1))
 
         offsets = keep.tile([P, S // 16], U16, name="offsets")
@@ -117,23 +116,22 @@ def tile_list_tabres_gelu_kernel(tc, tab_words, tab_scales, w, rT, b, offs, out)
                 bias=bias[:],
             )
 
-        picked_resid = {}
+        picked_resid = [keep.tile([M, N_TILE], F32, name="picked_resid%d" % i) for i in range(TILES)]
         result = [keep.tile([M, N_TILE], F32, name="result%d" % i) for i in range(TILES)]
 
         def gather_resid(i):
-            picked_resid[i] = ring.tile([M, N_TILE], F32, name="picked_resid")
             nc.vector.tensor_copy(picked_resid[i][:], resid[:].indirect(offs_of(i)))
 
-        def add_and_store(i, lo, hi, queue):
-            nc.vector.tensor_tensor(
+        def add_and_store(i, lo, hi, engine, queue):
+            engine.tensor_tensor(
                 result[i][:, lo:hi], picked_resid[i][:, lo:hi], act[i][:, lo:hi], mybir.AluOpType.add
             )
             queue.dma_start(out=out[:, i * N_TILE + lo : i * N_TILE + hi], in_=result[i][:, lo:hi])
 
         gather_resid(0)
+        add_and_store(0, 0, N_TILE, nc.gpsimd, nc.sync)
         gather_resid(1)
-        add_and_store(0, 0, N_TILE, nc.sync)
+        add_and_store(1, 0, N_TILE, nc.gpsimd, nc.sync)
         gather_resid(2)
-        add_and_store(1, 0, N_TILE, nc.sync)
-        add_and_store(2, 0, N_TILE // 2, nc.scalar)
-        add_and_store(2, N_TILE // 2, N_TILE, nc.sync)
+        add_and_store(2, 0, N_TILE // 2, nc.vector, nc.scalar)
+        add_and_store(2, N_TILE // 2, N_TILE, nc.vector, nc.sync)

@@ -40,6 +40,10 @@ def tile_list_tabres_gelu_kernel(tc, tab_words, tab_scales, w, rT, b, offs, out)
             rows = tab_words[a].rearrange("p t i -> p (t i)").bitcast(I32)
             nc.sync.dma_start(out=words[a][:, lo:hi], in_=rows[:, lo:hi])
 
+        def load_weight(a):
+            rows = w.rearrange("(a p j) n -> a p (j n)", a=PASSES, j=PACK)
+            nc.sync.dma_start(out=w_raw[:, a].rearrange("p j n -> p (j n)"), in_=rows[a])
+
         def load_scales(rows):
             for r in rows:
                 for a in range(PASSES):
@@ -49,10 +53,9 @@ def tile_list_tabres_gelu_kernel(tc, tab_words, tab_scales, w, rT, b, offs, out)
                     )
 
         nc.vector.memset(scale_tab[:], 0)
+        load_weight(0)
         nc.sync.dma_start(offsets[:], offs)
-        w_rows = w.rearrange("(a p j) n -> a p (j n)", a=PASSES, j=PACK)
-        for a in range(PASSES):
-            nc.sync.dma_start(out=w_raw[:, a].rearrange("p j n -> p (j n)"), in_=w_rows[a])
+        load_weight(1)
         load_scales((0, 1))
         load_words(0, 0, HEAD)
         load_scales((2, 3))
@@ -85,8 +88,7 @@ def tile_list_tabres_gelu_kernel(tc, tab_words, tab_scales, w, rT, b, offs, out)
             in_=w_bf[:].rearrange("p a n j -> p (a n j)"),
         )
 
-        for i in range(TILES):
-            nc.vector.tensor_copy(picked_scales[:, cols(i)], scale_tab[:].bitcast(U8).indirect(offs_of(i)))
+        nc.vector.tensor_copy(picked_scales[:], scale_tab[:].bitcast(U8).indirect(offsets[:]))
         nc.vector.tensor_copy(picked[0][:], words[0][:].bitcast(U32).indirect(offsets[:]))
 
         acc = [psum.tile([M, N_TILE], F32, name="acc%d" % i) for i in range(TILES)]
@@ -128,10 +130,12 @@ def tile_list_tabres_gelu_kernel(tc, tab_words, tab_scales, w, rT, b, offs, out)
             )
             queue.dma_start(out=out[:, i * N_TILE + lo : i * N_TILE + hi], in_=result[i][:, lo:hi])
 
+        half = N_TILE // 2
         gather_resid(0)
         add_and_store(0, 0, N_TILE, nc.gpsimd, nc.sync)
         gather_resid(1)
-        add_and_store(1, 0, N_TILE, nc.gpsimd, nc.sync)
+        add_and_store(1, 0, half, nc.gpsimd, nc.sync)
         gather_resid(2)
-        add_and_store(2, 0, N_TILE // 2, nc.vector, nc.scalar)
-        add_and_store(2, N_TILE // 2, N_TILE, nc.vector, nc.sync)
+        add_and_store(1, half, N_TILE, nc.vector, nc.scalar)
+        add_and_store(2, 0, half, nc.vector, nc.sync)
+        add_and_store(2, half, N_TILE, nc.vector, nc.scalar)

@@ -40,10 +40,6 @@ def tile_list_tabres_gelu_kernel(tc, tab_words, tab_scales, w, rT, b, offs, out)
             rows = tab_words[a].rearrange("p t i -> p (t i)").bitcast(I32)
             nc.sync.dma_start(out=words[a][:, lo:hi], in_=rows[:, lo:hi])
 
-        def load_weight(a):
-            rows = w.rearrange("(a p j) n -> a p (j n)", a=PASSES, j=PACK)
-            nc.sync.dma_start(out=w_raw[:, a].rearrange("p j n -> p (j n)"), in_=rows[a])
-
         def load_scales(rows):
             for r in rows:
                 for a in range(PASSES):
@@ -53,16 +49,18 @@ def tile_list_tabres_gelu_kernel(tc, tab_words, tab_scales, w, rT, b, offs, out)
                     )
 
         nc.vector.memset(scale_tab[:], 0)
-        load_weight(0)
+        nc.scalar.dma_start(out=bias[:], in_=b.rearrange("(p o) -> p o", o=1))
+        nc.sync.dma_start(
+            out=w_raw[:].rearrange("p a j n -> p a (j n)"),
+            in_=w.rearrange("(a p j) n -> p a (j n)", a=PASSES, j=PACK),
+        )
         nc.sync.dma_start(offsets[:], offs)
-        load_weight(1)
         load_scales((0, 1))
         load_words(0, 0, HEAD)
         load_scales((2, 3))
         load_words(0, HEAD, T)
         load_words(1, 0, T)
         nc.sync.dma_start(out=resid[:], in_=rT)
-        nc.sync.dma_start(out=bias[:], in_=b.rearrange("(p o) -> p o", o=1))
 
         warm_in = keep.tile([P, 1], F32, name="warm_in")
         warm_out = keep.tile([P, 1], F32, name="warm_out")
@@ -118,24 +116,15 @@ def tile_list_tabres_gelu_kernel(tc, tab_words, tab_scales, w, rT, b, offs, out)
                 bias=bias[:],
             )
 
-        picked_resid = [keep.tile([M, N_TILE], F32, name="picked_resid%d" % i) for i in range(TILES)]
-        result = [keep.tile([M, N_TILE], F32, name="result%d" % i) for i in range(TILES)]
-
-        def gather_resid(i):
-            nc.vector.tensor_copy(picked_resid[i][:], resid[:].indirect(offs_of(i)))
-
-        def add_and_store(i, lo, hi, engine, queue):
-            engine.tensor_tensor(
-                result[i][:, lo:hi], picked_resid[i][:, lo:hi], act[i][:, lo:hi], mybir.AluOpType.add
+        result = keep.tile([M, S], F32, name="result")
+        pieces = ((0, 512), (512, 1024), (1024, 1280), (1280, 1536))
+        for n, (lo, hi) in enumerate(pieces):
+            i = lo // N_TILE
+            nc.vector.tensor_tensor(
+                result[:, lo:hi],
+                resid[:].indirect(offsets[:, lo // 16 : hi // 16]),
+                act[i][:, lo - i * N_TILE : hi - i * N_TILE],
+                mybir.AluOpType.add,
             )
-            queue.dma_start(out=out[:, i * N_TILE + lo : i * N_TILE + hi], in_=result[i][:, lo:hi])
-
-        half = N_TILE // 2
-        gather_resid(0)
-        add_and_store(0, 0, N_TILE, nc.gpsimd, nc.sync)
-        gather_resid(1)
-        add_and_store(1, 0, half, nc.gpsimd, nc.sync)
-        gather_resid(2)
-        add_and_store(1, half, N_TILE, nc.vector, nc.scalar)
-        add_and_store(2, 0, half, nc.vector, nc.sync)
-        add_and_store(2, half, N_TILE, nc.vector, nc.scalar)
+            queue = nc.sync if n % 2 == 0 else nc.scalar
+            queue.dma_start(out=out[:, lo:hi], in_=result[:, lo:hi])

@@ -20,7 +20,6 @@ N_TILE = 512
 TILES = S // N_TILE
 OFFS_COLS = N_TILE // 16
 ROWS = 4
-HEAD = 1024
 
 
 def tile_list_tabres_gelu_kernel(tc, tab_words, tab_scales, w, rT, b, offs, out):
@@ -40,14 +39,6 @@ def tile_list_tabres_gelu_kernel(tc, tab_words, tab_scales, w, rT, b, offs, out)
             rows = tab_words[a].rearrange("p t i -> p (t i)").bitcast(I32)
             nc.sync.dma_start(out=words[a][:, lo:hi], in_=rows[:, lo:hi])
 
-        def load_scales(rows):
-            for r in rows:
-                for a in range(PASSES):
-                    nc.sync.dma_start(
-                        out=scale_tab[ROWS * a + r : P : 32, :],
-                        in_=tab_scales[a, r : 16 : ROWS, :].bitcast(I32),
-                    )
-
         nc.vector.memset(scale_tab[:], 0)
         nc.scalar.dma_start(out=bias[:], in_=b.rearrange("(p o) -> p o", o=1))
         nc.sync.dma_start(
@@ -55,10 +46,9 @@ def tile_list_tabres_gelu_kernel(tc, tab_words, tab_scales, w, rT, b, offs, out)
             in_=w.rearrange("(a p j) n -> p a (j n)", a=PASSES, j=PACK),
         )
         nc.sync.dma_start(offsets[:], offs)
-        load_scales((0, 1))
-        load_words(0, 0, HEAD)
-        load_scales((2, 3))
-        load_words(0, HEAD, T)
+        for a in range(PASSES):
+            nc.sync.dma_start(out=scale_tab[ROWS * a : P : 8, :], in_=tab_scales[a].bitcast(I32))
+        load_words(0, 0, T)
         load_words(1, 0, T)
         nc.sync.dma_start(out=resid[:], in_=rT)
 
@@ -87,6 +77,15 @@ def tile_list_tabres_gelu_kernel(tc, tab_words, tab_scales, w, rT, b, offs, out)
         )
 
         nc.vector.tensor_copy(picked_scales[:], scale_tab[:].bitcast(U8).indirect(offsets[:]))
+        planes = keep.tile([P, S // 4], I32, name="planes", align_bytes=64)
+        picked_rows = picked_scales[:].bitcast(I32)
+        nc.vector.tensor_copy(planes[:], picked_rows)
+        for a in range(PASSES):
+            for r in range(1, ROWS):
+                nc.scalar.dma_start(
+                    out=planes[ROWS * a + r : P : 32, :],
+                    in_=picked_scales[ROWS * a + 8 * r : P : 32, :].bitcast(I32),
+                )
         nc.vector.tensor_copy(picked[0][:], words[0][:].bitcast(U32).indirect(offsets[:]))
 
         acc = [psum.tile([M, N_TILE], F32, name="acc%d" % i) for i in range(TILES)]
@@ -97,7 +96,7 @@ def tile_list_tabres_gelu_kernel(tc, tab_words, tab_scales, w, rT, b, offs, out)
                 lhsT=w_codes[:, a * M : (a + 1) * M].bitcast(FP8X4),
                 lhsT_scale=w_scales[:, a * M : (a + 1) * M],
                 rhs=picked[a][:, cols(i)].bitcast(FP8X4),
-                rhs_scale=picked_scales[ROWS * a : P, cols(i)],
+                rhs_scale=planes[ROWS * a : P, :].bitcast(U8)[:, cols(i)],
                 start=(a == 0),
                 stop=(a == PASSES - 1),
             )

@@ -50,7 +50,6 @@ def tile_list_tabres_gelu_kernel(tc, tab_words, tab_scales, w, rT, b, offs, out)
             nc.sync.dma_start(out=scale_tab[ROWS * a : P : 8, :], in_=tab_scales[a].bitcast(I32))
         load_words(0, 0, T)
         load_words(1, 0, T)
-        nc.sync.dma_start(out=resid[:], in_=rT)
 
         warm_in = keep.tile([P, 1], F32, name="warm_in")
         warm_out = keep.tile([P, 1], F32, name="warm_out")
@@ -82,10 +81,11 @@ def tile_list_tabres_gelu_kernel(tc, tab_words, tab_scales, w, rT, b, offs, out)
         nc.vector.tensor_copy(planes[:], picked_rows)
         for a in range(PASSES):
             for r in range(1, ROWS):
-                nc.scalar.dma_start(
+                nc.sync.dma_start(
                     out=planes[ROWS * a + r : P : 32, :],
                     in_=picked_scales[ROWS * a + 8 * r : P : 32, :].bitcast(I32),
                 )
+        nc.sync.dma_start(out=resid[:], in_=rT)
         nc.vector.tensor_copy(picked[0][:], words[0][:].bitcast(U32).indirect(offsets[:]))
 
         acc = [psum.tile([M, N_TILE], F32, name="acc%d" % i) for i in range(TILES)]

@@ -33,14 +33,16 @@ def tile_list_tabres_gelu_kernel(tc, tab_words, tab_scales, w, rT, b, offs, out)
         scale_tab = keep.tile([P, T // 4], I32, name="scale_tab", align_bytes=64)
         resid = keep.tile([P, T], F32, name="resid", align_bytes=64)
         w_raw = keep.tile([P, PASSES, PACK, M], F32, name="w_raw", align_bytes=64)
-        bias = keep.tile([P, 1], F32, name="bias")
 
         def load_words(a, lo, hi):
             rows = tab_words[a].rearrange("p t i -> p (t i)").bitcast(I32)
             nc.sync.dma_start(out=words[a][:, lo:hi], in_=rows[:, lo:hi])
 
+        bias_rows = keep.tile([P, 32], F32, name="bias_rows", align_bytes=64)
+        bias_cols = keep.tile([P, 32], F32, name="bias_cols", align_bytes=64)
+        nc.vector.memset(bias_rows[:], 0.0)
         nc.vector.memset(scale_tab[:], 0)
-        nc.scalar.dma_start(out=bias[:], in_=b.rearrange("(p o) -> p o", o=1))
+        nc.scalar.dma_start(out=bias_rows[0:P:32, :], in_=b.rearrange("(q i) -> q i", i=32))
         nc.sync.dma_start(
             out=w_raw[:].rearrange("p a j n -> p a (j n)"),
             in_=w.rearrange("(a p j) n -> p a (j n)", a=PASSES, j=PACK),
@@ -65,6 +67,7 @@ def tile_list_tabres_gelu_kernel(tc, tab_words, tab_scales, w, rT, b, offs, out)
         picked = [keep.tile([P, S], U32, name="picked%d" % a, align_bytes=64) for a in range(PASSES)]
         picked_scales = keep.tile([P, S], U8, name="picked_scales", align_bytes=64)
 
+        nc.vector.transpose(bias_cols[:], bias_rows[:])
         w_bf = keep.tile([P, PASSES, M, PACK], BF16, name="w_bf", align_bytes=64)
         nc.vector.tensor_copy(out=w_bf[:], in_=w_raw[:].rearrange("p a j n -> p a n j"))
         w_codes = keep.tile([P, PASSES * M], U32, name="w_codes", align_bytes=64)
@@ -112,11 +115,11 @@ def tile_list_tabres_gelu_kernel(tc, tab_words, tab_scales, w, rT, b, offs, out)
                 out=act[i][:],
                 in_=acc[i][:],
                 func=mybir.ActivationFunctionType.Gelu_apprx_tanh,
-                bias=bias[:],
+                bias=bias_cols[:, 0:1],
             )
 
         result = keep.tile([M, S], F32, name="result")
-        pieces = ((0, 512), (512, 1024), (1024, 1280), (1280, 1536))
+        pieces = ((0, 512), (512, 1024), (1024, 1408), (1408, 1536))
         for n, (lo, hi) in enumerate(pieces):
             i = lo // N_TILE
             nc.vector.tensor_tensor(
@@ -125,5 +128,5 @@ def tile_list_tabres_gelu_kernel(tc, tab_words, tab_scales, w, rT, b, offs, out)
                 act[i][:, lo - i * N_TILE : hi - i * N_TILE],
                 mybir.AluOpType.add,
             )
-            queue = nc.sync if n % 2 == 0 else nc.scalar
+            queue = nc.scalar if n % 2 == 0 else nc.sync
             queue.dma_start(out=out[:, lo:hi], in_=result[:, lo:hi])

@@ -69,7 +69,7 @@ def tile_list_tabres_gelu_kernel(tc, tab_words, tab_scales, w, rT, b, offs, out)
 
         nc.vector.transpose(bias_cols[:], bias_rows[:])
         w_bf = keep.tile([P, PASSES, M, PACK], BF16, name="w_bf", align_bytes=64)
-        nc.vector.tensor_copy(out=w_bf[:], in_=w_raw[:].rearrange("p a j n -> p a n j"))
+        nc.scalar.copy(out=w_bf[:], in_=w_raw[:].rearrange("p a j n -> p a n j"))
         w_codes = keep.tile([P, PASSES * M], U32, name="w_codes", align_bytes=64)
         w_scales = keep.tile([P, PASSES * M], U8, name="w_scales", align_bytes=64)
         nc.vector.quantize_mx(

@@ -107,25 +107,24 @@ def tile_list_tabres_gelu_kernel(tc, tab_words, tab_scales, w, rT, b, offs, out)
         for i in range(TILES):
             mx_pass(0, i)
 
-        act = [keep.tile([M, N_TILE], F32, name="act%d" % i) for i in range(TILES)]
+        act = keep.tile([M, S], F32, name="act")
         for i in range(TILES):
             nc.vector.tensor_copy(picked[1][:, cols(i)], words[1][:].bitcast(U32).indirect(offs_of(i)))
             mx_pass(1, i)
             nc.scalar.activation(
-                out=act[i][:],
+                out=act[:, cols(i)],
                 in_=acc[i][:],
                 func=mybir.ActivationFunctionType.Gelu_apprx_tanh,
                 bias=bias_cols[:, 0:1],
             )
 
         result = keep.tile([M, S], F32, name="result")
-        pieces = ((0, 512), (512, 1024), (1024, 1408), (1408, 1536))
+        pieces = ((0, 640), (640, 1152), (1152, 1408), (1408, 1536))
         for n, (lo, hi) in enumerate(pieces):
-            i = lo // N_TILE
             nc.vector.tensor_tensor(
                 result[:, lo:hi],
                 resid[:].indirect(offsets[:, lo // 16 : hi // 16]),
-                act[i][:, lo - i * N_TILE : hi - i * N_TILE],
+                act[:, lo:hi],
                 mybir.AluOpType.add,
             )
             queue = nc.scalar if n % 2 == 0 else nc.sync

@@ -42,12 +42,12 @@ def tile_list_tabres_gelu_kernel(tc, tab_words, tab_scales, w, rT, b, offs, out)
         bias_cols = keep.tile([P, 32], F32, name="bias_cols", align_bytes=64)
         nc.vector.memset(bias_rows[:], 0.0)
         nc.vector.memset(scale_tab[:], 0)
-        nc.scalar.dma_start(out=bias_rows[0:P:32, :], in_=b.rearrange("(q i) -> q i", i=32))
         nc.sync.dma_start(
             out=w_raw[:].rearrange("p a j n -> p a (j n)"),
             in_=w.rearrange("(a p j) n -> p a (j n)", a=PASSES, j=PACK),
         )
         nc.sync.dma_start(offsets[:], offs)
+        nc.sync.dma_start(out=bias_rows[0:P:32, :], in_=b.rearrange("(q i) -> q i", i=32))
         for a in range(PASSES):
             nc.sync.dma_start(out=scale_tab[ROWS * a : P : 8, :], in_=tab_scales[a].bitcast(I32))
         load_words(0, 0, T)
@@ -120,12 +120,11 @@ def tile_list_tabres_gelu_kernel(tc, tab_words, tab_scales, w, rT, b, offs, out)
 
         result = keep.tile([M, S], F32, name="result")
         pieces = ((0, 640), (640, 1152), (1152, 1408), (1408, 1536))
-        for n, (lo, hi) in enumerate(pieces):
+        for lo, hi in pieces:
             nc.vector.tensor_tensor(
                 result[:, lo:hi],
                 resid[:].indirect(offsets[:, lo // 16 : hi // 16]),
                 act[:, lo:hi],
                 mybir.AluOpType.add,
             )
-            queue = nc.scalar if n % 2 == 0 else nc.sync
-            queue.dma_start(out=out[:, lo:hi], in_=result[:, lo:hi])
+            nc.sync.dma_start(out=out[:, lo:hi], in_=result[:, lo:hi])

@@ -48,8 +48,7 @@ def tile_list_tabres_gelu_kernel(tc, tab_words, tab_scales, w, rT, b, offs, out)
         )
         nc.sync.dma_start(offsets[:], offs)
         nc.sync.dma_start(out=bias_rows[0:P:32, :], in_=b.rearrange("(q i) -> q i", i=32))
-        for a in range(PASSES):
-            nc.sync.dma_start(out=scale_tab[ROWS * a : P : 8, :], in_=tab_scales[a].bitcast(I32))
+        nc.sync.dma_start(out=scale_tab[0:P:ROWS, :], in_=tab_scales.bitcast(I32).rearrange("a q t -> q a t"))
         load_words(0, 0, T)
         load_words(1, 0, T)
 

@@ -52,11 +52,6 @@ def tile_list_tabres_gelu_kernel(tc, tab_words, tab_scales, w, rT, b, offs, out)
         load_words(0, 0, T)
         load_words(1, 0, T)
 
-        warm_in = keep.tile([P, 1], F32, name="warm_in")
-        warm_out = keep.tile([P, 1], F32, name="warm_out")
-        nc.vector.memset(warm_in[:], 0.0)
-        nc.scalar.activation(out=warm_out[:], in_=warm_in[:], func=mybir.ActivationFunctionType.Gelu_apprx_tanh)
-
         def cols(i):
             return slice(i * N_TILE, (i + 1) * N_TILE)
 
@@ -68,7 +63,7 @@ def tile_list_tabres_gelu_kernel(tc, tab_words, tab_scales, w, rT, b, offs, out)
 
         nc.vector.transpose(bias_cols[:], bias_rows[:])
         w_bf = keep.tile([P, PASSES, M, PACK], BF16, name="w_bf", align_bytes=64)
-        nc.scalar.copy(out=w_bf[:], in_=w_raw[:].rearrange("p a j n -> p a n j"))
+        nc.vector.tensor_copy(out=w_bf[:], in_=w_raw[:].rearrange("p a j n -> p a n j"))
         w_codes = keep.tile([P, PASSES * M], U32, name="w_codes", align_bytes=64)
         w_scales = keep.tile([P, PASSES * M], U8, name="w_scales", align_bytes=64)
         nc.vector.quantize_mx(

@@ -76,8 +76,8 @@ def tile_list_tabres_gelu_kernel(tc, tab_words, tab_scales, w, rT, b, offs, out)
         planes = keep.tile([P, S // 4], I32, name="planes", align_bytes=64)
         picked_rows = picked_scales[:].bitcast(I32)
         nc.vector.tensor_copy(planes[:], picked_rows)
-        for a in range(PASSES):
-            for r in range(1, ROWS):
+        for r in range(1, ROWS):
+            for a in range(PASSES):
                 nc.sync.dma_start(
                     out=planes[ROWS * a + r : P : 32, :],
                     in_=picked_scales[ROWS * a + 8 * r : P : 32, :].bitcast(I32),

@@ -40,15 +40,15 @@ def tile_list_tabres_gelu_kernel(tc, tab_words, tab_scales, w, rT, b, offs, out)
 
         bias_rows = keep.tile([P, 32], F32, name="bias_rows", align_bytes=64)
         bias_cols = keep.tile([P, 32], F32, name="bias_cols", align_bytes=64)
-        nc.vector.memset(bias_rows[:], 0.0)
         nc.vector.memset(scale_tab[:], 0)
+        nc.vector.memset(bias_rows[:], 0.0)
         nc.sync.dma_start(
             out=w_raw[:].rearrange("p a j n -> p a (j n)"),
             in_=w.rearrange("(a p j) n -> p a (j n)", a=PASSES, j=PACK),
         )
         nc.sync.dma_start(offsets[:], offs)
-        nc.sync.dma_start(out=bias_rows[0:P:32, :], in_=b.rearrange("(q i) -> q i", i=32))
         nc.sync.dma_start(out=scale_tab[0:P:ROWS, :], in_=tab_scales.bitcast(I32).rearrange("a q t -> q a t"))
+        nc.sync.dma_start(out=bias_rows[0:P:32, :], in_=b.rearrange("(q i) -> q i", i=32))
         load_words(0, 0, T)
         load_words(1, 0, T)
 
@@ -61,16 +61,10 @@ def tile_list_tabres_gelu_kernel(tc, tab_words, tab_scales, w, rT, b, offs, out)
         picked = [keep.tile([P, S], U32, name="picked%d" % a, align_bytes=64) for a in range(PASSES)]
         picked_scales = keep.tile([P, S], U8, name="picked_scales", align_bytes=64)
 
-        nc.vector.transpose(bias_cols[:], bias_rows[:])
         w_bf = keep.tile([P, PASSES, M, PACK], BF16, name="w_bf", align_bytes=64)
         nc.vector.tensor_copy(out=w_bf[:], in_=w_raw[:].rearrange("p a j n -> p a n j"))
         w_codes = keep.tile([P, PASSES * M], U32, name="w_codes", align_bytes=64)
         w_scales = keep.tile([P, PASSES * M], U8, name="w_scales", align_bytes=64)
-        nc.vector.quantize_mx(
-            out=w_codes[:].bitcast(FP8X4),
-            scales=w_scales[:],
-            in_=w_bf[:].rearrange("p a n j -> p (a n j)"),
-        )
 
         nc.vector.tensor_copy(picked_scales[:], scale_tab[:].bitcast(U8).indirect(offsets[:]))
         planes = keep.tile([P, S // 4], I32, name="planes", align_bytes=64)
@@ -83,6 +77,12 @@ def tile_list_tabres_gelu_kernel(tc, tab_words, tab_scales, w, rT, b, offs, out)
                     in_=picked_scales[ROWS * a + 8 * r : P : 32, :].bitcast(I32),
                 )
         nc.sync.dma_start(out=resid[:], in_=rT)
+        nc.vector.quantize_mx(
+            out=w_codes[:].bitcast(FP8X4),
+            scales=w_scales[:],
+            in_=w_bf[:].rearrange("p a n j -> p (a n j)"),
+        )
+        nc.vector.transpose(bias_cols[:], bias_rows[:])
         nc.vector.tensor_copy(picked[0][:], words[0][:].bitcast(U32).indirect(offsets[:]))
 
         acc = [psum.tile([M, N_TILE], F32, name="acc%d" % i) for i in range(TILES)]

@@ -28,18 +28,18 @@ def tile_list_tabres_gelu_kernel(tc, tab_words, tab_scales, w, rT, b, offs, out)
         keep = ctx.enter_context(tc.tile_pool(name="keep", bufs=1))
         psum = ctx.enter_context(tc.psum_pool(name="psum", bufs=1))
 
-        offsets = keep.tile([P, S // 16], U16, name="offsets")
-        words = [keep.tile([P, T], I32, name="words%d" % a, align_bytes=64) for a in range(PASSES)]
-        scale_tab = keep.tile([P, T // 4], I32, name="scale_tab", align_bytes=64)
-        resid = keep.tile([P, T], F32, name="resid", align_bytes=64)
-        w_raw = keep.tile([P, PASSES, PACK, M], F32, name="w_raw", align_bytes=64)
+        offsets = keep.tile([P, S // 16], U16, name="offsets", align_bytes=256)
+        words = [keep.tile([P, T], I32, name="words%d" % a, align_bytes=256) for a in range(PASSES)]
+        scale_tab = keep.tile([P, T // 4], I32, name="scale_tab", align_bytes=256)
+        resid = keep.tile([P, T], F32, name="resid", align_bytes=256)
+        w_raw = keep.tile([P, PASSES, PACK, M], F32, name="w_raw", align_bytes=256)
 
         def load_words(a, lo, hi):
             rows = tab_words[a].rearrange("p t i -> p (t i)").bitcast(I32)
             nc.sync.dma_start(out=words[a][:, lo:hi], in_=rows[:, lo:hi])
 
-        bias_rows = keep.tile([P, 32], F32, name="bias_rows", align_bytes=64)
-        bias_cols = keep.tile([P, 32], F32, name="bias_cols", align_bytes=64)
+        bias_rows = keep.tile([P, 32], F32, name="bias_rows", align_bytes=256)
+        bias_cols = keep.tile([P, 32], F32, name="bias_cols", align_bytes=256)
         nc.vector.memset(scale_tab[:], 0)
         nc.vector.memset(bias_rows[:], 0.0)
         nc.sync.dma_start(
@@ -58,16 +58,16 @@ def tile_list_tabres_gelu_kernel(tc, tab_words, tab_scales, w, rT, b, offs, out)
         def offs_of(i):
             return offsets[:, i * OFFS_COLS : (i + 1) * OFFS_COLS]
 
-        picked = [keep.tile([P, S], U32, name="picked%d" % a, align_bytes=64) for a in range(PASSES)]
-        picked_scales = keep.tile([P, S], U8, name="picked_scales", align_bytes=64)
+        picked = [keep.tile([P, S], U32, name="picked%d" % a, align_bytes=256) for a in range(PASSES)]
+        picked_scales = keep.tile([P, S], U8, name="picked_scales", align_bytes=256)
 
-        w_bf = keep.tile([P, PASSES, M, PACK], BF16, name="w_bf", align_bytes=64)
+        w_bf = keep.tile([P, PASSES, M, PACK], BF16, name="w_bf", align_bytes=256)
         nc.vector.tensor_copy(out=w_bf[:], in_=w_raw[:].rearrange("p a j n -> p a n j"))
-        w_codes = keep.tile([P, PASSES * M], U32, name="w_codes", align_bytes=64)
-        w_scales = keep.tile([P, PASSES * M], U8, name="w_scales", align_bytes=64)
+        w_codes = keep.tile([P, PASSES * M], U32, name="w_codes", align_bytes=256)
+        w_scales = keep.tile([P, PASSES * M], U8, name="w_scales", align_bytes=256)
 
         nc.vector.tensor_copy(picked_scales[:], scale_tab[:].bitcast(U8).indirect(offsets[:]))
-        planes = keep.tile([P, S // 4], I32, name="planes", align_bytes=64)
+        planes = keep.tile([P, S // 4], I32, name="planes", align_bytes=256)
         picked_rows = picked_scales[:].bitcast(I32)
         nc.vector.tensor_copy(planes[:], picked_rows)
         for r in range(1, ROWS):
@@ -101,7 +101,7 @@ def tile_list_tabres_gelu_kernel(tc, tab_words, tab_scales, w, rT, b, offs, out)
         for i in range(TILES):
             mx_pass(0, i)
 
-        act = keep.tile([M, S], F32, name="act")
+        act = keep.tile([M, S], F32, name="act", align_bytes=256)
         for i in range(TILES):
             nc.vector.tensor_copy(picked[1][:, cols(i)], words[1][:].bitcast(U32).indirect(offs_of(i)))
             mx_pass(1, i)
@@ -112,7 +112,7 @@ def tile_list_tabres_gelu_kernel(tc, tab_words, tab_scales, w, rT, b, offs, out)
                 bias=bias_cols[:, 0:1],
             )
 
-        result = keep.tile([M, S], F32, name="result")
+        result = keep.tile([M, S], F32, name="result", align_bytes=256)
         pieces = ((0, 640), (640, 1152), (1152, 1408), (1408, 1536))
         for lo, hi in pieces:
             nc.vector.tensor_tensor(

@@ -29,10 +29,10 @@ def tile_list_tabres_gelu_kernel(tc, tab_words, tab_scales, w, rT, b, offs, out)
         psum = ctx.enter_context(tc.psum_pool(name="psum", bufs=1))
 
         offsets = keep.tile([P, S // 16], U16, name="offsets", align_bytes=256)
-        words = [keep.tile([P, T], I32, name="words%d" % a, align_bytes=256) for a in range(PASSES)]
-        scale_tab = keep.tile([P, T // 4], I32, name="scale_tab", align_bytes=256)
-        resid = keep.tile([P, T], F32, name="resid", align_bytes=256)
-        w_raw = keep.tile([P, PASSES, PACK, M], F32, name="w_raw", align_bytes=256)
+        words = [keep.tile([P, T], I32, name="words%d" % a, align_bytes=4096) for a in range(PASSES)]
+        scale_tab = keep.tile([P, T // 4], I32, name="scale_tab", align_bytes=4096)
+        resid = keep.tile([P, T], F32, name="resid", align_bytes=4096)
+        w_raw = keep.tile([P, PASSES, PACK, M], F32, name="w_raw", align_bytes=4096)
 
         def load_words(a, lo, hi):
             rows = tab_words[a].rearrange("p t i -> p (t i)").bitcast(I32)
@@ -112,7 +112,7 @@ def tile_list_tabres_gelu_kernel(tc, tab_words, tab_scales, w, rT, b, offs, out)
                 bias=bias_cols[:, 0:1],
             )
 
-        result = keep.tile([M, S], F32, name="result", align_bytes=256)
+        result = keep.tile([M, S], F32, name="result", align_bytes=4096)
         pieces = ((0, 640), (640, 1152), (1152, 1408), (1408, 1536))
         for lo, hi in pieces:
             nc.vector.tensor_tensor(

@@ -20,6 +20,8 @@ N_TILE = 512
 TILES = S // N_TILE
 OFFS_COLS = N_TILE // 16
 ROWS = 4
+LATE = 1024
+CHUNKS = ((0, 512), (512, 1024), (1024, 1280), (1280, 1536))
 
 
 def tile_list_tabres_gelu_kernel(tc, tab_words, tab_scales, w, rT, b, offs, out):
@@ -67,16 +69,23 @@ def tile_list_tabres_gelu_kernel(tc, tab_words, tab_scales, w, rT, b, offs, out)
         w_scales = keep.tile([P, PASSES * M], U8, name="w_scales", align_bytes=256)
 
         nc.vector.tensor_copy(picked_scales[:], scale_tab[:].bitcast(U8).indirect(offsets[:]))
-        planes = keep.tile([P, S // 4], I32, name="planes", align_bytes=256)
         picked_rows = picked_scales[:].bitcast(I32)
-        nc.vector.tensor_copy(planes[:], picked_rows)
-        for r in range(1, ROWS):
-            for a in range(PASSES):
-                nc.sync.dma_start(
-                    out=planes[ROWS * a + r : P : 32, :],
-                    in_=picked_scales[ROWS * a + 8 * r : P : 32, :].bitcast(I32),
-                )
+        planes = {}
+
+        def move_rows(lo, hi):
+            plane = keep.tile([P, (hi - lo) // 4], I32, name="planes%d" % lo, align_bytes=256)
+            nc.vector.tensor_copy(plane[:], picked_rows[:, lo // 4 : hi // 4])
+            for r in range(1, ROWS):
+                for a in range(PASSES):
+                    nc.sync.dma_start(
+                        out=plane[ROWS * a + r : P : 32, :],
+                        in_=picked_scales[ROWS * a + 8 * r : P : 32, lo:hi].bitcast(I32),
+                    )
+            planes[lo] = plane
+
+        move_rows(0, LATE)
         nc.sync.dma_start(out=resid[:], in_=rT)
+        move_rows(LATE, S)
         nc.vector.quantize_mx(
             out=w_codes[:].bitcast(FP8X4),
             scales=w_scales[:],
@@ -85,35 +94,36 @@ def tile_list_tabres_gelu_kernel(tc, tab_words, tab_scales, w, rT, b, offs, out)
         nc.vector.transpose(bias_cols[:], bias_rows[:])
         nc.vector.tensor_copy(picked[0][:], words[0][:].bitcast(U32).indirect(offsets[:]))
 
-        acc = [psum.tile([M, N_TILE], F32, name="acc%d" % i) for i in range(TILES)]
+        acc = [psum.tile([M, N_TILE], F32, name="acc%d" % i) for i in range(len(CHUNKS))]
 
         def mx_pass(a, i):
+            lo, hi = CHUNKS[i]
+            base = 0 if lo < LATE else LATE
             nc.tensor.matmul_mx(
-                out=acc[i][:],
+                out=acc[i][:, 0 : hi - lo],
                 lhsT=w_codes[:, a * M : (a + 1) * M].bitcast(FP8X4),
                 lhsT_scale=w_scales[:, a * M : (a + 1) * M],
-                rhs=picked[a][:, cols(i)].bitcast(FP8X4),
-                rhs_scale=planes[ROWS * a : P, :].bitcast(U8)[:, cols(i)],
+                rhs=picked[a][:, lo:hi].bitcast(FP8X4),
+                rhs_scale=planes[base][ROWS * a : P, :].bitcast(U8)[:, lo - base : hi - base],
                 start=(a == 0),
                 stop=(a == PASSES - 1),
             )
 
-        for i in range(TILES):
-            mx_pass(0, i)
-
         act = keep.tile([M, S], F32, name="act", align_bytes=256)
         for i in range(TILES):
             nc.vector.tensor_copy(picked[1][:, cols(i)], words[1][:].bitcast(U32).indirect(offs_of(i)))
-            mx_pass(1, i)
+        for i, (lo, hi) in enumerate(CHUNKS):
+            for a in range(PASSES):
+                mx_pass(a, i)
             nc.scalar.activation(
-                out=act[:, cols(i)],
-                in_=acc[i][:],
+                out=act[:, lo:hi],
+                in_=acc[i][:, 0 : hi - lo],
                 func=mybir.ActivationFunctionType.Gelu_apprx_tanh,
                 bias=bias_cols[:, 0:1],
             )
 
         result = keep.tile([M, S], F32, name="result", align_bytes=4096)
-        pieces = ((0, 640), (640, 1152), (1152, 1408), (1408, 1536))
+        pieces = ((0, 512), (512, 960), (960, 1344), (1344, 1536))
         for lo, hi in pieces:
             nc.vector.tensor_tensor(
                 result[:, lo:hi],

@@ -20,8 +20,8 @@ N_TILE = 512
 TILES = S // N_TILE
 OFFS_COLS = N_TILE // 16
 ROWS = 4
-LATE = 1024
-CHUNKS = ((0, 512), (512, 1024), (1024, 1280), (1280, 1536))
+LATE = (1024, 768)
+CHUNKS = ((0, 512), (512, 768), (768, 1024), (1024, 1280), (1280, 1536))
 
 
 def tile_list_tabres_gelu_kernel(tc, tab_words, tab_scales, w, rT, b, offs, out):
@@ -72,20 +72,28 @@ def tile_list_tabres_gelu_kernel(tc, tab_words, tab_scales, w, rT, b, offs, out)
         picked_rows = picked_scales[:].bitcast(I32)
         planes = {}
 
-        def move_rows(lo, hi):
-            plane = keep.tile([P, (hi - lo) // 4], I32, name="planes%d" % lo, align_bytes=256)
+        def copy_rows(a, lo, hi):
+            plane = keep.tile([P, (hi - lo) // 4], I32, name="planes%d_%d" % (a, lo), align_bytes=256)
             nc.vector.tensor_copy(plane[:], picked_rows[:, lo // 4 : hi // 4])
-            for r in range(1, ROWS):
-                for a in range(PASSES):
-                    nc.sync.dma_start(
-                        out=plane[ROWS * a + r : P : 32, :],
-                        in_=picked_scales[ROWS * a + 8 * r : P : 32, lo:hi].bitcast(I32),
-                    )
-            planes[lo] = plane
+            planes[a, lo] = plane
 
-        move_rows(0, LATE)
+        def move_row(a, r, lo, hi):
+            nc.sync.dma_start(
+                out=planes[a, lo][ROWS * a + r : P : 32, :],
+                in_=picked_scales[ROWS * a + 8 * r : P : 32, lo:hi].bitcast(I32),
+            )
+
+        for a in range(PASSES):
+            copy_rows(a, 0, LATE[a])
+        for a in range(PASSES):
+            copy_rows(a, LATE[a], S)
+        for r in range(1, ROWS):
+            for a in range(PASSES):
+                move_row(a, r, 0, LATE[a])
         nc.sync.dma_start(out=resid[:], in_=rT)
-        move_rows(LATE, S)
+        for a in reversed(range(PASSES)):
+            for r in range(1, ROWS):
+                move_row(a, r, LATE[a], S)
         nc.vector.quantize_mx(
             out=w_codes[:].bitcast(FP8X4),
             scales=w_scales[:],
@@ -96,24 +104,27 @@ def tile_list_tabres_gelu_kernel(tc, tab_words, tab_scales, w, rT, b, offs, out)
 
         acc = [psum.tile([M, N_TILE], F32, name="acc%d" % i) for i in range(len(CHUNKS))]
 
+        def order(i):
+            return (0, 1) if CHUNKS[i][0] < LATE[0] else (1, 0)
+
         def mx_pass(a, i):
             lo, hi = CHUNKS[i]
-            base = 0 if lo < LATE else LATE
+            base = 0 if lo < LATE[a] else LATE[a]
             nc.tensor.matmul_mx(
                 out=acc[i][:, 0 : hi - lo],
                 lhsT=w_codes[:, a * M : (a + 1) * M].bitcast(FP8X4),
                 lhsT_scale=w_scales[:, a * M : (a + 1) * M],
                 rhs=picked[a][:, lo:hi].bitcast(FP8X4),
-                rhs_scale=planes[base][ROWS * a : P, :].bitcast(U8)[:, lo - base : hi - base],
-                start=(a == 0),
-                stop=(a == PASSES - 1),
+                rhs_scale=planes[a, base][ROWS * a : P, :].bitcast(U8)[:, lo - base : hi - base],
+                start=(a == order(i)[0]),
+                stop=(a == order(i)[-1]),
             )
 
         act = keep.tile([M, S], F32, name="act", align_bytes=256)
         for i in range(TILES):
             nc.vector.tensor_copy(picked[1][:, cols(i)], words[1][:].bitcast(U32).indirect(offs_of(i)))
         for i, (lo, hi) in enumerate(CHUNKS):
-            for a in range(PASSES):
+            for a in order(i):
                 mx_pass(a, i)
             nc.scalar.activation(
                 out=act[:, lo:hi],
@@ -123,7 +134,7 @@ def tile_list_tabres_gelu_kernel(tc, tab_words, tab_scales, w, rT, b, offs, out)
             )
 
         result = keep.tile([M, S], F32, name="result", align_bytes=4096)
-        pieces = ((0, 512), (512, 960), (960, 1344), (1344, 1536))
+        pieces = ((0, 768),) + CHUNKS[2:]
         for lo, hi in pieces:
             nc.vector.tensor_tensor(
                 result[:, lo:hi],

@@ -21,7 +21,7 @@ TILES = S // N_TILE
 OFFS_COLS = N_TILE // 16
 ROWS = 4
 LATE = (1024, 768)
-CHUNKS = ((0, 512), (512, 768), (768, 1024), (1024, 1280), (1280, 1536))
+CHUNKS = ((0, 512), (512, 768), (768, 1024), (1024, 1280), (1280, 1408), (1408, 1536))
 
 
 def tile_list_tabres_gelu_kernel(tc, tab_words, tab_scales, w, rT, b, offs, out):
@@ -124,7 +124,10 @@ def tile_list_tabres_gelu_kernel(tc, tab_words, tab_scales, w, rT, b, offs, out)
         for i in range(TILES):
             nc.vector.tensor_copy(picked[1][:, cols(i)], words[1][:].bitcast(U32).indirect(offs_of(i)))
         for i, (lo, hi) in enumerate(CHUNKS):
-            for a in order(i):
+            if lo == LATE[0]:
+                for j in range(i, len(CHUNKS)):
+                    mx_pass(order(j)[0], j)
+            for a in order(i)[1 if lo >= LATE[0] else 0 :]:
                 mx_pass(a, i)
             nc.scalar.activation(
                 out=act[:, lo:hi],
@@ -134,7 +137,7 @@ def tile_list_tabres_gelu_kernel(tc, tab_words, tab_scales, w, rT, b, offs, out)
             )
 
         result = keep.tile([M, S], F32, name="result", align_bytes=4096)
-        pieces = ((0, 768),) + CHUNKS[2:]
+        pieces = ((0, 640), (640, 1024), (1024, 1344), (1344, 1536))
         for lo, hi in pieces:
             nc.vector.tensor_tensor(
                 result[:, lo:hi],

@@ -21,7 +21,7 @@ TILES = S // N_TILE
 OFFS_COLS = N_TILE // 16
 ROWS = 4
 LATE = (1024, 768)
-CHUNKS = ((0, 512), (512, 768), (768, 1024), (1024, 1280), (1280, 1408), (1408, 1536))
+CHUNKS = ((0, 512), (512, 768), (768, 1024), (1024, 1152), (1152, 1408), (1408, 1536))
 
 
 def tile_list_tabres_gelu_kernel(tc, tab_words, tab_scales, w, rT, b, offs, out):
@@ -105,7 +105,7 @@ def tile_list_tabres_gelu_kernel(tc, tab_words, tab_scales, w, rT, b, offs, out)
         acc = [psum.tile([M, N_TILE], F32, name="acc%d" % i) for i in range(len(CHUNKS))]
 
         def order(i):
-            return (0, 1) if CHUNKS[i][0] < LATE[0] else (1, 0)
+            return (1, 0) if LATE[0] <= CHUNKS[i][0] and CHUNKS[i][1] < S else (0, 1)
 
         def mx_pass(a, i):
             lo, hi = CHUNKS[i]
@@ -125,9 +125,9 @@ def tile_list_tabres_gelu_kernel(tc, tab_words, tab_scales, w, rT, b, offs, out)
             nc.vector.tensor_copy(picked[1][:, cols(i)], words[1][:].bitcast(U32).indirect(offs_of(i)))
         for i, (lo, hi) in enumerate(CHUNKS):
             if lo == LATE[0]:
-                for j in range(i, len(CHUNKS)):
+                for j in range(i, len(CHUNKS) - 1):
                     mx_pass(order(j)[0], j)
-            for a in order(i)[1 if lo >= LATE[0] else 0 :]:
+            for a in order(i)[1 if LATE[0] <= lo and hi < S else 0 :]:
                 mx_pass(a, i)
             nc.scalar.activation(
                 out=act[:, lo:hi],
@@ -137,7 +137,7 @@ def tile_list_tabres_gelu_kernel(tc, tab_words, tab_scales, w, rT, b, offs, out)
             )
 
         result = keep.tile([M, S], F32, name="result", align_bytes=4096)
-        pieces = ((0, 640), (640, 1024), (1024, 1344), (1344, 1536))
+        pieces = ((0, 768), (768, 1152), (1152, 1408), (1408, 1536))
         for lo, hi in pieces:
             nc.vector.tensor_tensor(
                 result[:, lo:hi],

@@ -17,11 +17,12 @@ P = 128
 PACK = 4
 PASSES = K // (P * PACK)
 N_TILE = 512
-TILES = S // N_TILE
-OFFS_COLS = N_TILE // 16
 ROWS = 4
-LATE = (1024, 768)
-CHUNKS = ((0, 512), (512, 768), (768, 1024), (1024, 1152), (1152, 1408), (1408, 1536))
+LATE = (1024, 896)
+CHUNKS = ((0, 512), (512, 768), (768, 896), (896, 1024), (1024, 1152), (1152, 1408), (1408, 1536))
+PIECES = ((0, 768), (768, 1152), (1152, 1408), (1408, 1536))
+STAGED = (768, 896)
+SLICES = ((0, 896), (896, 1536))
 
 
 def tile_list_tabres_gelu_kernel(tc, tab_words, tab_scales, w, rT, b, offs, out):
@@ -53,12 +54,6 @@ def tile_list_tabres_gelu_kernel(tc, tab_words, tab_scales, w, rT, b, offs, out)
         nc.sync.dma_start(out=bias_rows[0:P:32, :], in_=b.rearrange("(q i) -> q i", i=32))
         load_words(0, 0, T)
         load_words(1, 0, T)
-
-        def cols(i):
-            return slice(i * N_TILE, (i + 1) * N_TILE)
-
-        def offs_of(i):
-            return offsets[:, i * OFFS_COLS : (i + 1) * OFFS_COLS]
 
         picked = [keep.tile([P, S], U32, name="picked%d" % a, align_bytes=256) for a in range(PASSES)]
         picked_scales = keep.tile([P, S], U8, name="picked_scales", align_bytes=256)
@@ -121,24 +116,27 @@ def tile_list_tabres_gelu_kernel(tc, tab_words, tab_scales, w, rT, b, offs, out)
             )
 
         act = keep.tile([M, S], F32, name="act", align_bytes=256)
-        for i in range(TILES):
-            nc.vector.tensor_copy(picked[1][:, cols(i)], words[1][:].bitcast(U32).indirect(offs_of(i)))
+        act_stage = keep.tile([M, STAGED[1] - STAGED[0]], F32, name="act_stage", align_bytes=256)
+        for lo, hi in SLICES:
+            nc.vector.tensor_copy(picked[1][:, lo:hi], words[1][:].bitcast(U32).indirect(offsets[:, lo // 16 : hi // 16]))
         for i, (lo, hi) in enumerate(CHUNKS):
             if lo == LATE[0]:
                 for j in range(i, len(CHUNKS) - 1):
                     mx_pass(order(j)[0], j)
             for a in order(i)[1 if LATE[0] <= lo and hi < S else 0 :]:
                 mx_pass(a, i)
+            staged = (lo, hi) == STAGED
             nc.scalar.activation(
-                out=act[:, lo:hi],
+                out=act_stage[:] if staged else act[:, lo:hi],
                 in_=acc[i][:, 0 : hi - lo],
                 func=mybir.ActivationFunctionType.Gelu_apprx_tanh,
                 bias=bias_cols[:, 0:1],
             )
+            if staged:
+                nc.vector.tensor_copy(act[:, lo:hi], act_stage[:])
 
         result = keep.tile([M, S], F32, name="result", align_bytes=4096)
-        pieces = ((0, 768), (768, 1152), (1152, 1408), (1408, 1536))
-        for lo, hi in pieces:
+        for lo, hi in PIECES:
             nc.vector.tensor_tensor(
                 result[:, lo:hi],
                 resid[:].indirect(offsets[:, lo // 16 : hi // 16]),

@@ -22,7 +22,7 @@ LATE = (1024, 896)
 CHUNKS = ((0, 512), (512, 768), (768, 896), (896, 1024), (1024, 1152), (1152, 1408), (1408, 1536))
 PIECES = ((0, 768), (768, 1152), (1152, 1408), (1408, 1536))
 STAGED = (768, 896)
-SLICES = ((0, 896), (896, 1536))
+SLICES = ((0, 512), (512, 1024), (1024, 1536))
 
 
 def tile_list_tabres_gelu_kernel(tc, tab_words, tab_scales, w, rT, b, offs, out):
@@ -120,10 +120,11 @@ def tile_list_tabres_gelu_kernel(tc, tab_words, tab_scales, w, rT, b, offs, out)
         for lo, hi in SLICES:
             nc.vector.tensor_copy(picked[1][:, lo:hi], words[1][:].bitcast(U32).indirect(offsets[:, lo // 16 : hi // 16]))
         for i, (lo, hi) in enumerate(CHUNKS):
-            if lo == LATE[0]:
+            if lo in (0, LATE[0]):
                 for j in range(i, len(CHUNKS) - 1):
-                    mx_pass(order(j)[0], j)
-            for a in order(i)[1 if LATE[0] <= lo and hi < S else 0 :]:
+                    if (CHUNKS[j][0] < LATE[0]) == (lo < LATE[0]):
+                        mx_pass(order(j)[0], j)
+            for a in order(i)[1 if hi < S else 0 :]:
                 mx_pass(a, i)
             staged = (lo, hi) == STAGED
             nc.scalar.activation(

@@ -18,10 +18,10 @@ PACK = 4
 PASSES = K // (P * PACK)
 N_TILE = 512
 ROWS = 4
-LATE = (1024, 896)
-CHUNKS = ((0, 512), (512, 768), (768, 896), (896, 1024), (1024, 1152), (1152, 1408), (1408, 1536))
-PIECES = ((0, 768), (768, 1152), (1152, 1408), (1408, 1536))
-STAGED = (768, 896)
+LATE = (1024, 768)
+CHUNKS = ((0, 512), (512, 768), (768, 1024), (1024, 1152), (1152, 1408), (1408, 1536))
+PIECES = ((0, 736), (736, 1152), (1152, 1408), (1408, 1536))
+STAGED = (736, 768)
 SLICES = ((0, 512), (512, 1024), (1024, 1536))
 
 
@@ -100,7 +100,7 @@ def tile_list_tabres_gelu_kernel(tc, tab_words, tab_scales, w, rT, b, offs, out)
         acc = [psum.tile([M, N_TILE], F32, name="acc%d" % i) for i in range(len(CHUNKS))]
 
         def order(i):
-            return (1, 0) if LATE[0] <= CHUNKS[i][0] and CHUNKS[i][1] < S else (0, 1)
+            return (1, 0) if CHUNKS[i][0] == LATE[0] else (0, 1)
 
         def mx_pass(a, i):
             lo, hi = CHUNKS[i]
@@ -115,26 +115,30 @@ def tile_list_tabres_gelu_kernel(tc, tab_words, tab_scales, w, rT, b, offs, out)
                 stop=(a == order(i)[-1]),
             )
 
+        def gelu(dst, sums):
+            nc.scalar.activation(
+                out=dst,
+                in_=sums,
+                func=mybir.ActivationFunctionType.Gelu_apprx_tanh,
+                bias=bias_cols[:, 0:1],
+            )
+
         act = keep.tile([M, S], F32, name="act", align_bytes=256)
         act_stage = keep.tile([M, STAGED[1] - STAGED[0]], F32, name="act_stage", align_bytes=256)
         for lo, hi in SLICES:
             nc.vector.tensor_copy(picked[1][:, lo:hi], words[1][:].bitcast(U32).indirect(offsets[:, lo // 16 : hi // 16]))
         for i, (lo, hi) in enumerate(CHUNKS):
-            if lo in (0, LATE[0]):
-                for j in range(i, len(CHUNKS) - 1):
-                    if (CHUNKS[j][0] < LATE[0]) == (lo < LATE[0]):
-                        mx_pass(order(j)[0], j)
-            for a in order(i)[1 if hi < S else 0 :]:
+            if lo == 0:
+                for j in range(len(CHUNKS)):
+                    if CHUNKS[j][0] < LATE[0]:
+                        mx_pass(0, j)
+            for a in order(i)[1 if lo < LATE[0] else 0 :]:
                 mx_pass(a, i)
-            staged = (lo, hi) == STAGED
-            nc.scalar.activation(
-                out=act_stage[:] if staged else act[:, lo:hi],
-                in_=acc[i][:, 0 : hi - lo],
-                func=mybir.ActivationFunctionType.Gelu_apprx_tanh,
-                bias=bias_cols[:, 0:1],
-            )
-            if staged:
-                nc.vector.tensor_copy(act[:, lo:hi], act_stage[:])
+            end = STAGED[0] if hi == STAGED[1] else hi
+            gelu(act[:, lo:end], acc[i][:, 0 : end - lo])
+            if end < hi:
+                gelu(act_stage[:], acc[i][:, end - lo : hi - lo])
+                nc.vector.tensor_copy(act[:, end:hi], act_stage[:])
 
         result = keep.tile([M, S], F32, name="result", align_bytes=4096)
         for lo, hi in PIECES:

from contextlib import ExitStack

import concourse.mybir as mybir

K, M, T, S = 1024, 128, 4096, 1536
FLOPS = 2 * K * M * S

F32 = mybir.dt.float32
BF16 = mybir.dt.bfloat16
I32 = mybir.dt.int32
U32 = mybir.dt.uint32
U16 = mybir.dt.uint16
U8 = mybir.dt.uint8
FP8X4 = mybir.dt.float8_e4m3fn_x4

P = 128
PACK = 4
PASSES = K // (P * PACK)
N_TILE = 512
ROWS = 4
LATE = (1024, 768)
CHUNKS = ((0, 512), (512, 768), (768, 1024), (1024, 1152), (1152, 1408), (1408, 1536))
PIECES = ((0, 736), (736, 1152), (1152, 1408), (1408, 1536))
STAGED = (736, 768)
SLICES = ((0, 512), (512, 1024), (1024, 1536))


def tile_list_tabres_gelu_kernel(tc, tab_words, tab_scales, w, rT, b, offs, out):
    nc = tc.nc
    with ExitStack() as ctx:
        keep = ctx.enter_context(tc.tile_pool(name="keep", bufs=1))
        psum = ctx.enter_context(tc.psum_pool(name="psum", bufs=1))

        offsets = keep.tile([P, S // 16], U16, name="offsets", align_bytes=256)
        words = [keep.tile([P, T], I32, name="words%d" % a, align_bytes=4096) for a in range(PASSES)]
        scale_tab = keep.tile([P, T // 4], I32, name="scale_tab", align_bytes=4096)
        resid = keep.tile([P, T], F32, name="resid", align_bytes=4096)
        w_raw = keep.tile([P, PASSES, PACK, M], F32, name="w_raw", align_bytes=4096)

        def load_words(a, lo, hi):
            rows = tab_words[a].rearrange("p t i -> p (t i)").bitcast(I32)
            nc.sync.dma_start(out=words[a][:, lo:hi], in_=rows[:, lo:hi])

        bias_rows = keep.tile([P, 32], F32, name="bias_rows", align_bytes=256)
        bias_cols = keep.tile([P, 32], F32, name="bias_cols", align_bytes=256)
        nc.vector.memset(scale_tab[:], 0)
        nc.vector.memset(bias_rows[:], 0.0)
        nc.sync.dma_start(
            out=w_raw[:].rearrange("p a j n -> p a (j n)"),
            in_=w.rearrange("(a p j) n -> p a (j n)", a=PASSES, j=PACK),
        )
        nc.sync.dma_start(offsets[:], offs)
        nc.sync.dma_start(out=scale_tab[0:P:ROWS, :], in_=tab_scales.bitcast(I32).rearrange("a q t -> q a t"))
        nc.sync.dma_start(out=bias_rows[0:P:32, :], in_=b.rearrange("(q i) -> q i", i=32))
        load_words(0, 0, T)
        load_words(1, 0, T)

        picked = [keep.tile([P, S], U32, name="picked%d" % a, align_bytes=256) for a in range(PASSES)]
        picked_scales = keep.tile([P, S], U8, name="picked_scales", align_bytes=256)

        w_bf = keep.tile([P, PASSES, M, PACK], BF16, name="w_bf", align_bytes=256)
        nc.vector.tensor_copy(out=w_bf[:], in_=w_raw[:].rearrange("p a j n -> p a n j"))
        w_codes = keep.tile([P, PASSES * M], U32, name="w_codes", align_bytes=256)
        w_scales = keep.tile([P, PASSES * M], U8, name="w_scales", align_bytes=256)

        nc.vector.tensor_copy(picked_scales[:], scale_tab[:].bitcast(U8).indirect(offsets[:]))
        picked_rows = picked_scales[:].bitcast(I32)
        planes = {}

        def copy_rows(a, lo, hi):
            plane = keep.tile([P, (hi - lo) // 4], I32, name="planes%d_%d" % (a, lo), align_bytes=256)
            nc.vector.tensor_copy(plane[:], picked_rows[:, lo // 4 : hi // 4])
            planes[a, lo] = plane

        def move_row(a, r, lo, hi):
            nc.sync.dma_start(
                out=planes[a, lo][ROWS * a + r : P : 32, :],
                in_=picked_scales[ROWS * a + 8 * r : P : 32, lo:hi].bitcast(I32),
            )

        for a in range(PASSES):
            copy_rows(a, 0, LATE[a])
        for a in range(PASSES):
            copy_rows(a, LATE[a], S)
        for r in range(1, ROWS):
            for a in range(PASSES):
                move_row(a, r, 0, LATE[a])
        nc.sync.dma_start(out=resid[:], in_=rT)
        for a in reversed(range(PASSES)):
            for r in range(1, ROWS):
                move_row(a, r, LATE[a], S)
        nc.vector.quantize_mx(
            out=w_codes[:].bitcast(FP8X4),
            scales=w_scales[:],
            in_=w_bf[:].rearrange("p a n j -> p (a n j)"),
        )
        nc.vector.transpose(bias_cols[:], bias_rows[:])
        nc.vector.tensor_copy(picked[0][:], words[0][:].bitcast(U32).indirect(offsets[:]))

        acc = [psum.tile([M, N_TILE], F32, name="acc%d" % i) for i in range(len(CHUNKS))]

        def order(i):
            return (1, 0) if CHUNKS[i][0] == LATE[0] else (0, 1)

        def mx_pass(a, i):
            lo, hi = CHUNKS[i]
            base = 0 if lo < LATE[a] else LATE[a]
            nc.tensor.matmul_mx(
                out=acc[i][:, 0 : hi - lo],
                lhsT=w_codes[:, a * M : (a + 1) * M].bitcast(FP8X4),
                lhsT_scale=w_scales[:, a * M : (a + 1) * M],
                rhs=picked[a][:, lo:hi].bitcast(FP8X4),
                rhs_scale=planes[a, base][ROWS * a : P, :].bitcast(U8)[:, lo - base : hi - base],
                start=(a == order(i)[0]),
                stop=(a == order(i)[-1]),
            )

        def gelu(dst, sums):
            nc.scalar.activation(
                out=dst,
                in_=sums,
                func=mybir.ActivationFunctionType.Gelu_apprx_tanh,
                bias=bias_cols[:, 0:1],
            )

        act = keep.tile([M, S], F32, name="act", align_bytes=256)
        act_stage = keep.tile([M, STAGED[1] - STAGED[0]], F32, name="act_stage", align_bytes=256)
        for lo, hi in SLICES:
            nc.vector.tensor_copy(picked[1][:, lo:hi], words[1][:].bitcast(U32).indirect(offsets[:, lo // 16 : hi // 16]))
        for i, (lo, hi) in enumerate(CHUNKS):
            if lo == 0:
                for j in range(len(CHUNKS)):
                    if CHUNKS[j][0] < LATE[0]:
                        mx_pass(0, j)
            for a in order(i)[1 if lo < LATE[0] else 0 :]:
                mx_pass(a, i)
            end = STAGED[0] if hi == STAGED[1] else hi
            gelu(act[:, lo:end], acc[i][:, 0 : end - lo])
            if end < hi:
                gelu(act_stage[:], acc[i][:, end - lo : hi - lo])
                nc.vector.tensor_copy(act[:, end:hi], act_stage[:])

        result = keep.tile([M, S], F32, name="result", align_bytes=4096)
        for lo, hi in PIECES:
            nc.vector.tensor_tensor(
                result[:, lo:hi],
                resid[:].indirect(offsets[:, lo // 16 : hi // 16]),
                act[:, lo:hi],
                mybir.AluOpType.add,
            )
            nc.sync.dma_start(out=out[:, lo:hi], in_=result[:, lo:hi])
